import numpy as np
import ml_dtypes

BF16 = ml_dtypes.bfloat16


def bf(x):
    return np.asarray(x, np.float32).astype(BF16)


def f32(x):
    return np.asarray(x, np.float32)


def f64(x):
    return np.asarray(x).astype(np.float64)


def striped(idx):
    return np.tile(idx.reshape(-1, 16).T, (8, 1))


def rows(idx, k):
    return np.tile(idx, (k, 1))


K, S, V, N = 256, 2048, 512, 512


def setup_inputs():
    return {"base": bf(np.random.standard_normal((K, S))), "v": bf(np.random.standard_normal((K, V))), "offs": striped(np.random.permutation(S)[:N])}


def reference(base, v, offs):
    idx = offs[:16].T.reshape(-1)
    x = f64(base).copy()
    np.put_along_axis(x, rows(idx, len(x)), f64(v), axis=1)
    return x

@@ -1,0 +1,29 @@
+import concourse.mybir as mybir
+
+P = 128
+BF16, F32, U16 = mybir.dt.bfloat16, mybir.dt.float32, mybir.dt.uint16
+
+
+def tile_lookup_put_copy_out_kernel(tc, base, v, offs, out):
+    nc = tc.nc
+    rows, columns = base.shape
+    entries = v.shape[1]
+    blocks = rows // P
+
+    with (
+        tc.tile_pool(name="held", bufs=1) as held,
+        tc.tile_pool(name="block", bufs=blocks) as block_pool,
+    ):
+        offsets = held.tile(list(offs.shape), U16, name="offsets")
+        nc.sync.dma_start(offsets[:], offs)
+
+        for b in range(blocks):
+            block_rows = slice(b * P, (b + 1) * P)
+            x = block_pool.tile([P, columns], BF16, name="x")
+            values = block_pool.tile([P, entries], BF16, name="values")
+            wide = block_pool.tile([P, columns], F32, name="wide")
+            nc.sync.dma_start(x[:], base[block_rows, :])
+            nc.sync.dma_start(values[:], v[block_rows, :])
+            nc.vector.tensor_copy(x[:].indirect(offsets[:]), values[:])
+            nc.scalar.copy(wide[:], x[:])
+            nc.sync.dma_start(out[block_rows, :], wide[:])

@@ -3,27 +3,41 @@ import concourse.mybir as mybir
 P = 128
 BF16, F32, U16 = mybir.dt.bfloat16, mybir.dt.float32, mybir.dt.uint16
 
+LOAD_COLUMNS = 1024
+STORE_COLUMNS = 512
+
 
 def tile_lookup_put_copy_out_kernel(tc, base, v, offs, out):
     nc = tc.nc
-    rows, columns = base.shape
+    columns = base.shape[1]
     entries = v.shape[1]
-    blocks = rows // P
+    first_rows, second_rows = slice(0, P), slice(P, 2 * P)
 
-    with (
-        tc.tile_pool(name="held", bufs=1) as held,
-        tc.tile_pool(name="block", bufs=blocks) as block_pool,
-    ):
-        offsets = held.tile(list(offs.shape), U16, name="offsets")
+    with tc.tile_pool(name="sbuf", bufs=1) as pool:
+        offsets = pool.tile(list(offs.shape), U16, name="offsets")
+        first_x = pool.tile([P, columns], BF16, name="first_x")
+        first_v = pool.tile([P, entries], BF16, name="first_v")
+        second_v = pool.tile([P, entries], BF16, name="second_v")
+        second_base = pool.tile([P, columns], BF16, name="second_base", tag="scalar_work")
+        second_x = pool.tile([P, columns], F32, name="second_x")
+        second_v_wide = pool.tile([P, entries], F32, name="second_v_wide")
+
+        nc.sync.dma_start(first_x[:], base[first_rows, :])
+        nc.sync.dma_start(first_v[:], v[first_rows, :])
         nc.sync.dma_start(offsets[:], offs)
+        nc.vector.tensor_copy(first_x[:].indirect(offsets[:]), first_v[:])
 
-        for b in range(blocks):
-            block_rows = slice(b * P, (b + 1) * P)
-            x = block_pool.tile([P, columns], BF16, name="x")
-            values = block_pool.tile([P, entries], BF16, name="values")
-            wide = block_pool.tile([P, columns], F32, name="wide")
-            nc.sync.dma_start(x[:], base[block_rows, :])
-            nc.sync.dma_start(values[:], v[block_rows, :])
-            nc.vector.tensor_copy(x[:].indirect(offsets[:]), values[:])
-            nc.scalar.copy(wide[:], x[:])
-            nc.sync.dma_start(out[block_rows, :], wide[:])
+        nc.sync.dma_start(second_v[:], v[second_rows, :])
+        nc.scalar.copy(second_v_wide[:], second_v[:])
+        for start in range(0, columns, LOAD_COLUMNS):
+            piece = slice(start, start + LOAD_COLUMNS)
+            nc.sync.dma_start(second_base[:, piece], base[second_rows, piece])
+            nc.scalar.copy(second_x[:, piece], second_base[:, piece])
+        nc.vector.tensor_copy(second_x[:].indirect(offsets[:]), second_v_wide[:])
+
+        first_wide = pool.tile([P, columns], F32, name="first_wide", tag="scalar_work")
+        for start in range(0, columns, STORE_COLUMNS):
+            piece = slice(start, start + STORE_COLUMNS)
+            nc.scalar.copy(first_wide[:, piece], first_x[:, piece])
+            nc.scalar.dma_start(out[first_rows, piece], first_wide[:, piece])
+        nc.sync.dma_start(out[second_rows, :], second_x[:])

import concourse.mybir as mybir

P = 128
BF16, F32, U16 = mybir.dt.bfloat16, mybir.dt.float32, mybir.dt.uint16

LOAD_COLUMNS = 1024
STORE_COLUMNS = 512


def tile_lookup_put_copy_out_kernel(tc, base, v, offs, out):
    nc = tc.nc
    columns = base.shape[1]
    entries = v.shape[1]
    first_rows, second_rows = slice(0, P), slice(P, 2 * P)

    with tc.tile_pool(name="sbuf", bufs=1) as pool:
        offsets = pool.tile(list(offs.shape), U16, name="offsets")
        first_x = pool.tile([P, columns], BF16, name="first_x")
        first_v = pool.tile([P, entries], BF16, name="first_v")
        second_v = pool.tile([P, entries], BF16, name="second_v")
        second_base = pool.tile([P, columns], BF16, name="second_base", tag="scalar_work")
        second_x = pool.tile([P, columns], F32, name="second_x")
        second_v_wide = pool.tile([P, entries], F32, name="second_v_wide")

        nc.sync.dma_start(first_x[:], base[first_rows, :])
        nc.sync.dma_start(first_v[:], v[first_rows, :])
        nc.sync.dma_start(offsets[:], offs)
        nc.vector.tensor_copy(first_x[:].indirect(offsets[:]), first_v[:])

        nc.sync.dma_start(second_v[:], v[second_rows, :])
        nc.scalar.copy(second_v_wide[:], second_v[:])
        for start in range(0, columns, LOAD_COLUMNS):
            piece = slice(start, start + LOAD_COLUMNS)
            nc.sync.dma_start(second_base[:, piece], base[second_rows, piece])
            nc.scalar.copy(second_x[:, piece], second_base[:, piece])
        nc.vector.tensor_copy(second_x[:].indirect(offsets[:]), second_v_wide[:])

        first_wide = pool.tile([P, columns], F32, name="first_wide", tag="scalar_work")
        for start in range(0, columns, STORE_COLUMNS):
            piece = slice(start, start + STORE_COLUMNS)
            nc.scalar.copy(first_wide[:, piece], first_x[:, piece])
            nc.scalar.dma_start(out[first_rows, piece], first_wide[:, piece])
        nc.sync.dma_start(out[second_rows, :], second_x[:])
